import numpy as np
import ml_dtypes


def mxq(x, axis, fmt="e4m3"):
    dtype, down = {"e4m3": (ml_dtypes.float8_e4m3fn, 7), "e5m2": (ml_dtypes.float8_e5m2, 14)}[fmt]
    v = np.moveaxis(np.asarray(x, np.float32).astype(ml_dtypes.bfloat16).astype(np.float64), axis, -1)
    blocks = v.reshape(v.shape[:-1] + (-1, 32))
    amax = np.abs(blocks).max(-1, keepdims=True)
    byte = np.maximum(np.where(amax > 0, np.frexp(amax)[1] - 1 + 127, 0) - down, 1)
    scale = np.exp2(byte - 127.0)
    codes = (blocks / scale).astype(np.float32).astype(dtype).astype(np.float64)
    return np.moveaxis((codes * scale).reshape(v.shape), -1, axis)


WIDE = False


def mx_kscale(k):
    if not WIDE:
        return np.ones(k)
    levels = np.array([10, -10, 5, -5, 0])
    if k % 512:
        return np.exp2(np.random.permutation(np.resize(levels, k // 32))).repeat(32)
    a = np.empty((k // 512, 16))
    for p in range(k // 512):
        a[p, :8] = np.random.permutation(np.resize(levels, 8))
        for g in range(8):
            far = levels[np.abs(levels - a[p, g]) >= 10]
            a[p, g + 8] = far[np.random.randint(len(far))]
    return np.exp2(a.ravel()).repeat(32)


def f64(x):
    return np.asarray(x).astype(np.float64)


def striped(idx):
    return np.tile(idx.reshape(-1, 16).T, (8, 1)).astype(np.uint16)


def unstriped(offs):
    return offs[:16].T.reshape(-1).astype(np.int64)


def striped8(idx):
    return np.concatenate([x.reshape(-1, 16).T for x in idx]).astype(np.uint16)


def runs(offs, k):
    lists = np.stack([offs[16 * r : 16 * r + 16].T.reshape(-1) for r in range(8)]).astype(np.int64)
    return lists[np.arange(k) % 512 // 64]


def pack_weight(w):
    k, n = w.shape
    w = f64(np.asarray(w, np.float32).astype(ml_dtypes.bfloat16)).reshape(k // 32, 32, n)
    amax = np.abs(w).max(1)
    byte = np.clip(np.where(amax > 0, np.frexp(amax)[1] - 1 + 127 - 7, 1), 1, 254)
    scaled = (w * np.exp2(127.0 - byte)[:, None, :]).reshape(k, n).astype(np.float32)
    words = np.ascontiguousarray(scaled.reshape(k // 512, 128, 4, n).transpose(0, 1, 3, 2)).astype(ml_dtypes.float8_e4m3fn).view(np.uint8)
    return words, np.ascontiguousarray(byte.astype(np.uint8).reshape(k // 512, 16, n))


def unpack_weight(words, scales):
    g, p, n, _ = words.shape
    vals = np.ascontiguousarray(words).view(ml_dtypes.float8_e4m3fn).astype(np.float64) * np.repeat(np.exp2(scales.astype(np.float64) - 127.0), 8, axis=1)[..., None]
    return vals.transpose(0, 1, 3, 2).reshape(g * 512, n)


def sigmoid(v):
    return 1.0 / (1.0 + np.exp(-np.maximum(v, -700.0)))


K, T, S, N, G, H = 512, 2048, 512, 512, 2048, 512


def setup_inputs():
    n = np.random.standard_normal
    s = mx_kscale(K)[:, None]
    u = mx_kscale(S)
    packed_xT = pack_weight(n((K, T)) * s)
    packed_dT = pack_weight(n((K, G)) / s)
    return {
        "x_words": packed_xT[0],
        "x_scales": packed_xT[1],
        "d_words": packed_dT[0],
        "d_scales": packed_dT[1],
        "gn": (np.random.uniform(0.5, 1.5, (H, 1)) * u[:, None]).astype(np.float32),
        "w1": (n((H, N)) / np.sqrt(H) / u[:, None]).astype(np.float32),
        "offs": striped(np.random.permutation(T)[:S]),
        "k1": striped8(np.random.randint(0, G, (8, H))),
        "two": striped(np.random.permutation(T)[:S]),
        "n1": striped(np.random.permutation(S)),
        "n2": striped(np.random.permutation(S)),
        "n3": striped8(np.stack([np.random.permutation(S) for _ in range(8)])),
    }


def reference(x_words, x_scales, d_words, d_scales, gn, w1, offs, k1, two, n1, n2, n3):
    d_k1 = unpack_weight(d_words, d_scales)[np.arange(K)[:, None], runs(k1, K)]
    xq = unpack_weight(x_words, x_scales)[:, unstriped(offs)]
    a = 0.0625 * (d_k1.T @ xq)
    x_two = unpack_weight(x_words, x_scales)[:, unstriped(two)]
    b = 0.0625 * (d_k1.T @ x_two)
    z = f64(gn) * (a + (sigmoid(b[:, unstriped(n2)] - b)) * (a[:, unstriped(n1)] - a))
    h = mxq(f64(w1), 0, "e4m3").T @ mxq(z, 0, "e4m3")
    return np.maximum(h, h[np.arange(N)[:, None], runs(n3, N)])

@@ -1,0 +1,190 @@
+from contextlib import ExitStack
+
+import concourse.mybir as mybir
+from concourse.masks import make_identity
+
+F32 = mybir.dt.float32
+BF16 = mybir.dt.bfloat16
+I32 = mybir.dt.int32
+U32 = mybir.dt.uint32
+U16 = mybir.dt.uint16
+U8 = mybir.dt.uint8
+FP8X4 = mybir.dt.float8_e4m3fn_x4
+ACT = mybir.ActivationFunctionType
+ALU = mybir.AluOpType
+
+P = 128
+S = 512
+T = 2048
+NT = 4
+FLOPS = 3 * 2 * 512 * 512 * 512
+CHUNKS = ((0, 256), (256, 512))
+SHIFT = 14
+
+
+def tile_picked_twkspullbbig_none_p_kernel(tc, x_words, x_scales, d_words, d_scales, gn, w1, offs, k1, two, n1, n2, n3, out):
+    nc = tc.nc
+    with ExitStack() as ctx:
+        keep = ctx.enter_context(tc.tile_pool(name="keep", bufs=1))
+        work = ctx.enter_context(tc.tile_pool(name="work", bufs=2))
+        psum = ctx.enter_context(tc.psum_pool(name="psum", bufs=2))
+        psum1 = ctx.enter_context(tc.psum_pool(name="psum1", bufs=1))
+        psum4 = ctx.enter_context(tc.psum_pool(name="psum4", bufs=4))
+
+        def load_list(src, name):
+            t = keep.tile([P, S // 16], U16, name=name)
+            nc.sync.dma_start(t[:], src)
+            return t
+
+        dsc = keep.tile([P, T], U8, name="dsc", align_bytes=64)
+        xsc = keep.tile([P, T], U8, name="xsc", align_bytes=64)
+        dw = keep.tile([P, T], U32, name="dw", align_bytes=64)
+        xw = keep.tile([P, T], U32, name="xw", align_bytes=64)
+        key_sc = keep.tile([P, S], U8, name="key_sc", align_bytes=64)
+        nc.vector.memset(dsc[:].bitcast(I32), 0)
+        nc.vector.memset(xsc[:].bitcast(I32), 0)
+        nc.vector.memset(key_sc[:].bitcast(I32), 0)
+
+        k1_t = load_list(k1, "k1_t")
+        two_t = load_list(two, "two_t")
+        for q in range(4):
+            nc.scalar.dma_start(dsc[32 * q + SHIFT : 32 * q + SHIFT + 4, :].bitcast(I32), d_scales[0, 4 * q : 4 * q + 4, :].bitcast(I32))
+        nc.sync.dma_start(dw[:].bitcast(I32), d_words[0].rearrange("p n t -> p (n t)").bitcast(I32))
+        nc.sync.dma_start(xw[:].bitcast(I32), x_words[0].rearrange("p n t -> p (n t)").bitcast(I32))
+        for q in range(4):
+            nc.scalar.dma_start(xsc[32 * q : 32 * q + 4, :].bitcast(I32), x_scales[0, 4 * q : 4 * q + 4, :].bitcast(I32))
+        offs_t = load_list(offs, "offs_t")
+        w_raw = keep.tile([P, 4, S], F32, name="w_raw")
+        nc.sync.dma_start(w_raw[:], w1.rearrange("(p j) c -> p j c", j=4))
+        n2_t = load_list(n2, "n2_t")
+        gain = keep.tile([P, NT], F32, name="gain")
+        nc.sync.dma_start(gain[:], gn.rearrange("(p t) o -> p (t o)", t=NT))
+        n1_t = load_list(n1, "n1_t")
+        n3_t = load_list(n3, "n3_t")
+
+        ident = keep.tile([P, P], F32, name="ident")
+        make_identity(nc, ident[:])
+
+        ksc_g = keep.tile([P, S], U8, name="ksc_g", align_bytes=64)
+        nc.vector.tensor_copy(ksc_g[:], dsc[:].indirect(k1_t[:]))
+        ksc_d = keep.tile([P, S], U8, name="ksc_d", align_bytes=64)
+        nc.vector.tensor_copy(ksc_d[:].rearrange("p (t a b) -> p a t b", t=NT, b=16), ksc_g[:].rearrange("p (a b t) -> p a t b", t=NT, b=16))
+        nc.scalar.dma_start(key_sc[0:100, :].bitcast(I32), ksc_d[SHIFT : SHIFT + 100, :].bitcast(I32))
+
+        bsc = keep.tile([P, S], U8, name="bsc", align_bytes=64)
+        nc.vector.tensor_copy(bsc[:], xsc[:].indirect(two_t[:]))
+        kw_g = keep.tile([P, S], U32, name="kw_g", align_bytes=64)
+        nc.vector.tensor_copy(kw_g[:], dw[:].indirect(k1_t[:]))
+        key_w = keep.tile([P, S], U32, name="key_w", align_bytes=64)
+        nc.vector.tensor_copy(key_w[:].rearrange("p (t a b) -> p a t b", t=NT, b=4), kw_g[:].rearrange("p (a b t) -> p a t b", t=NT, b=4))
+        asc = keep.tile([P, S], U8, name="asc", align_bytes=64)
+        nc.vector.tensor_copy(asc[:], xsc[:].indirect(offs_t[:]))
+        bw = keep.tile([P, S], U32, name="bw", align_bytes=64)
+        nc.vector.tensor_copy(bw[:], xw[:].indirect(two_t[:]))
+        aw = keep.tile([P, S], U32, name="aw", align_bytes=64)
+        nc.vector.tensor_copy(aw[:], xw[:].indirect(offs_t[:]))
+
+        def blk(i):
+            return slice(i * P, (i + 1) * P)
+
+        def mm(dst, lw, ls, rw, rs):
+            nc.tensor.matmul_mx(out=dst, lhsT=lw.bitcast(FP8X4), lhsT_scale=ls, rhs=rw.bitcast(FP8X4), rhs_scale=rs, start=True, stop=True)
+
+        w_bf = keep.tile([P, NT, P, 4], BF16, name="w_bf", align_bytes=64)
+        for t in range(NT):
+            nc.gpsimd.tensor_copy(w_bf[:, t, :, :], w_raw[:].rearrange("p j (m t) -> p t m j", t=NT)[:, t, :, :])
+        w_q = keep.tile([P, S], U32, name="w_q", align_bytes=64)
+        w_s = keep.tile([P, S], U8, name="w_s", align_bytes=64)
+
+        b_sb = [keep.tile([P, S], F32, name="b_sb%d" % t) for t in range(NT)]
+        a_sb = keep.tile([P, NT, S], F32, name="a_sb")
+        bg = keep.tile([P, NT, S], F32, name="bg")
+        ag = keep.tile([P, NT, S], F32, name="ag")
+        z_q = keep.tile([P, S], U32, name="z_q", align_bytes=64)
+        z_s = keep.tile([P, S], U8, name="z_s", align_bytes=64)
+        h_sb = [keep.tile([P, S], F32, name="h_sb%d" % t) for t in range(NT)]
+
+        def diff_t(bank, own, neg, t, jb):
+            nc.tensor.matmul(bank[:, t, :], own[:, blk(jb)], ident[:], start=True, stop=False, is_transpose=True)
+            nc.tensor.matmul(bank[:, t, :], neg[:, blk(jb)], ident[:], start=False, stop=True, is_transpose=True)
+
+        def gather_neg(dst, window, lst, lo, hi):
+            nc.scalar.activation(out=dst[:, lo:hi], in_=window.indirect(lst[:, lo // 16 : hi // 16]), func=ACT.Copy, scale=-1.0)
+
+        for t in range(NT):
+            ps = psum4.tile([P, S], F32, name="dd")
+            mm(ps[:], key_w[:, blk(t)], key_sc[:, blk(t)], bw[:], bsc[:])
+            if t < 1:
+                nc.scalar.copy(b_sb[t][:], ps[:])
+            else:
+                nc.vector.tensor_copy(b_sb[t][:], ps[:])
+        for t in range(NT):
+            ps = psum.tile([P, S], F32, name="zz") if t < 2 else psum1.tile([P, S], F32, name=("ee", "aa")[t - 2])
+            mm(ps[:], key_w[:, blk(t)], key_sc[:, blk(t)], aw[:], asc[:])
+            nc.vector.tensor_scalar(a_sb[:, t, :], ps[:], gain[:, t : t + 1], 0.0625, ALU.mult, ALU.mult)
+        nc.vector.quantize_mx(out=w_q[:].bitcast(FP8X4), scales=w_s[:], in_=w_bf[:].rearrange("p t m j -> p (t m j)"))
+
+        dbank = [psum4.tile([P, NT, P], F32, name="dd") for jb in range(NT)]
+        for t in range(NT):
+            for lo, hi in CHUNKS:
+                gather_neg(bg[:, t, :], b_sb[t][:], n2_t, lo, hi)
+                for jb in range(lo // P, hi // P):
+                    diff_t(dbank[jb], b_sb[t], bg[:, t, :], t, jb)
+        sg = [keep.tile([P, NT, P], F32, name="sg%d" % jb) for jb in range(NT)]
+        ebank = {}
+        zb = {}
+        hbank = []
+
+        def pull(jb):
+            ebank[jb] = psum1.tile([P, NT, P], F32, name="ee")
+            for t in range(NT):
+                gather_neg(ag[:, t, :], a_sb[:, t, :], n1_t, jb * P, (jb + 1) * P)
+                diff_t(ebank[jb], a_sb[:, t, :], ag[:, t, :], t, jb)
+
+        def gate(jb):
+            nc.scalar.activation(out=sg[jb][:], in_=dbank[jb][:], func=ACT.Sigmoid, scale=-0.0625)
+
+        def weigh(jb):
+            mt = work.tile([P, NT, P], F32, name="mt")
+            nc.vector.tensor_tensor(mt[:], ebank[jb][:], sg[jb][:], ALU.mult)
+            zb[jb] = psum.tile([P, NT, P], F32, name="zz")
+            for t in range(NT):
+                nc.tensor.transpose(zb[jb][:, t, :], mt[:, t, :], ident[:])
+
+        def finish(jb):
+            zf = work.tile([P, P, NT], BF16, name="zf", align_bytes=64)
+            nc.vector.tensor_tensor(zf[:], a_sb[:, :, blk(jb)].rearrange("p t j -> p j t"), zb[jb][:].rearrange("p t j -> p j t"), ALU.subtract)
+            nc.vector.quantize_mx(out=z_q[:, blk(jb)].bitcast(FP8X4), scales=z_s[:, blk(jb)], in_=zf[:].rearrange("p j t -> p (j t)"))
+            for t in range(NT):
+                mm(hbank[t][:, blk(jb)], w_q[:, blk(t)], w_s[:, blk(t)], z_q[:, blk(jb)], z_s[:, blk(jb)])
+
+        pull(0)
+        gate(0)
+        gate(1)
+        weigh(0)
+        pull(1)
+        gate(2)
+        gate(3)
+        hbank.extend(psum4.tile([P, S], F32, name="dd") for t in range(NT))
+        finish(0)
+        weigh(1)
+        pull(2)
+        finish(1)
+        weigh(2)
+        pull(3)
+        finish(2)
+        nc.vector.tensor_copy(h_sb[0][:, 0:384], hbank[0][:, 0:384])
+        weigh(3)
+        finish(3)
+        nc.vector.tensor_copy(h_sb[0][:, 384:512], hbank[0][:, 384:512])
+
+        rows = out.rearrange("(p t) j -> p t j", t=NT)
+        for t in range(NT):
+            if t + 1 < NT:
+                nc.vector.tensor_copy(h_sb[t + 1][:], hbank[t + 1][:])
+            hg = keep.tile([P, S], F32, name="hg%d" % t)
+            res = keep.tile([P, S], F32, name="res%d" % t)
+            for lo, hi in ((0, 256), (256, 512)):
+                nc.scalar.activation(out=hg[:, lo:hi], in_=h_sb[t][:].indirect(n3_t[:, lo // 16 : hi // 16]), func=ACT.Copy)
+                nc.vector.tensor_tensor(res[:, lo:hi], hg[:, lo:hi], h_sb[t][:, lo:hi], ALU.max)
+                nc.sync.dma_start(rows[:, t, lo:hi], res[:, lo:hi])

@@ -1,7 +1,6 @@
 from contextlib import ExitStack
 
 import concourse.mybir as mybir
-from concourse.masks import make_identity
 
 F32 = mybir.dt.float32
 BF16 = mybir.dt.bfloat16
@@ -18,17 +17,13 @@ S = 512
 T = 2048
 NT = 4
 FLOPS = 3 * 2 * 512 * 512 * 512
-CHUNKS = ((0, 256), (256, 512))
-SHIFT = 14
+HALF = 256
 
 
 def tile_picked_twkspullbbig_none_p_kernel(tc, x_words, x_scales, d_words, d_scales, gn, w1, offs, k1, two, n1, n2, n3, out):
     nc = tc.nc
     with ExitStack() as ctx:
         keep = ctx.enter_context(tc.tile_pool(name="keep", bufs=1))
-        work = ctx.enter_context(tc.tile_pool(name="work", bufs=2))
-        psum = ctx.enter_context(tc.psum_pool(name="psum", bufs=2))
-        psum1 = ctx.enter_context(tc.psum_pool(name="psum1", bufs=1))
         psum4 = ctx.enter_context(tc.psum_pool(name="psum4", bufs=4))
 
         def load_list(src, name):
@@ -41,19 +36,17 @@ def tile_picked_twkspullbbig_none_p_kernel(tc, x_words, x_scales, d_words, d_sca
         dw = keep.tile([P, T], U32, name="dw", align_bytes=64)
         xw = keep.tile([P, T], U32, name="xw", align_bytes=64)
         key_sc = keep.tile([P, S], U8, name="key_sc", align_bytes=64)
-        nc.vector.memset(dsc[:].bitcast(I32), 0)
+        nc.gpsimd.memset(dsc[:].bitcast(I32), 0)
         nc.vector.memset(xsc[:].bitcast(I32), 0)
-        nc.vector.memset(key_sc[:].bitcast(I32), 0)
 
         k1_t = load_list(k1, "k1_t")
         two_t = load_list(two, "two_t")
-        for q in range(4):
-            nc.scalar.dma_start(dsc[32 * q + SHIFT : 32 * q + SHIFT + 4, :].bitcast(I32), d_scales[0, 4 * q : 4 * q + 4, :].bitcast(I32))
-        nc.sync.dma_start(dw[:].bitcast(I32), d_words[0].rearrange("p n t -> p (n t)").bitcast(I32))
-        nc.sync.dma_start(xw[:].bitcast(I32), x_words[0].rearrange("p n t -> p (n t)").bitcast(I32))
+        offs_t = load_list(offs, "offs_t")
+        nc.scalar.dma_start(dsc[0:P:8, :].bitcast(I32), d_scales[0].bitcast(I32))
         for q in range(4):
             nc.scalar.dma_start(xsc[32 * q : 32 * q + 4, :].bitcast(I32), x_scales[0, 4 * q : 4 * q + 4, :].bitcast(I32))
-        offs_t = load_list(offs, "offs_t")
+        nc.sync.dma_start(dw[:].bitcast(I32), d_words[0].rearrange("p n t -> p (n t)").bitcast(I32))
+        nc.sync.dma_start(xw[:].bitcast(I32), x_words[0].rearrange("p n t -> p (n t)").bitcast(I32))
         w_raw = keep.tile([P, 4, S], F32, name="w_raw")
         nc.sync.dma_start(w_raw[:], w1.rearrange("(p j) c -> p j c", j=4))
         n2_t = load_list(n2, "n2_t")
@@ -62,14 +55,12 @@ def tile_picked_twkspullbbig_none_p_kernel(tc, x_words, x_scales, d_words, d_sca
         n1_t = load_list(n1, "n1_t")
         n3_t = load_list(n3, "n3_t")
 
-        ident = keep.tile([P, P], F32, name="ident")
-        make_identity(nc, ident[:])
 
         ksc_g = keep.tile([P, S], U8, name="ksc_g", align_bytes=64)
         nc.vector.tensor_copy(ksc_g[:], dsc[:].indirect(k1_t[:]))
-        ksc_d = keep.tile([P, S], U8, name="ksc_d", align_bytes=64)
-        nc.vector.tensor_copy(ksc_d[:].rearrange("p (t a b) -> p a t b", t=NT, b=16), ksc_g[:].rearrange("p (a b t) -> p a t b", t=NT, b=16))
-        nc.scalar.dma_start(key_sc[0:100, :].bitcast(I32), ksc_d[SHIFT : SHIFT + 100, :].bitcast(I32))
+        nc.vector.tensor_copy(key_sc[:].rearrange("p (t a b) -> p a t b", t=NT, b=16), ksc_g[:].rearrange("p (a b t) -> p a t b", t=NT, b=16))
+        for j in range(1, 4):
+            nc.scalar.dma_start(key_sc[j:P:32, :].bitcast(I32), key_sc[8 * j : P : 32, :].bitcast(I32))
 
         bsc = keep.tile([P, S], U8, name="bsc", align_bytes=64)
         nc.vector.tensor_copy(bsc[:], xsc[:].indirect(two_t[:]))
@@ -96,87 +87,134 @@ def tile_picked_twkspullbbig_none_p_kernel(tc, x_words, x_scales, d_words, d_sca
         w_q = keep.tile([P, S], U32, name="w_q", align_bytes=64)
         w_s = keep.tile([P, S], U8, name="w_s", align_bytes=64)
 
-        b_sb = [keep.tile([P, S], F32, name="b_sb%d" % t) for t in range(NT)]
+        b_sb = keep.tile([P, NT, S], F32, name="b_sb")
         a_sb = keep.tile([P, NT, S], F32, name="a_sb")
-        bg = keep.tile([P, NT, S], F32, name="bg")
-        ag = keep.tile([P, NT, S], F32, name="ag")
+        dif = keep.tile([P, NT, S], F32, name="dif")
+        pull = keep.tile([P, NT, S], F32, name="pull")
+        step = keep.tile([P, NT, S], F32, name="step")
+        z_bf = keep.tile([P, S, NT], BF16, name="z_bf", align_bytes=64)
         z_q = keep.tile([P, S], U32, name="z_q", align_bytes=64)
         z_s = keep.tile([P, S], U8, name="z_s", align_bytes=64)
         h_sb = [keep.tile([P, S], F32, name="h_sb%d" % t) for t in range(NT)]
+        g16 = keep.tile([P, NT], F32, name="g16")
+        nc.gpsimd.tensor_scalar(g16[:], gain[:], 0.0625, 0.0, ALU.mult, ALU.add)
 
-        def diff_t(bank, own, neg, t, jb):
-            nc.tensor.matmul(bank[:, t, :], own[:, blk(jb)], ident[:], start=True, stop=False, is_transpose=True)
-            nc.tensor.matmul(bank[:, t, :], neg[:, blk(jb)], ident[:], start=False, stop=True, is_transpose=True)
+        def pair_buffer(tag, u):
+            return keep.tile([P, 2, HALF], F32, name="%s%d" % (tag, u))
 
-        def gather_neg(dst, window, lst, lo, hi):
-            nc.scalar.activation(out=dst[:, lo:hi], in_=window.indirect(lst[:, lo // 16 : hi // 16]), func=ACT.Copy, scale=-1.0)
+        def gather(dst, window, lst, lo, hi, scale):
+            nc.scalar.activation(out=dst, in_=window.indirect(lst[:, lo // 16 : hi // 16]), func=ACT.Copy, scale=scale)
 
+        b_ps = [psum4.tile([P, S], F32, name="bh") for t in range(NT)]
+        a_ps = [psum4.tile([P, S], F32, name="aa") for t in range(NT)]
         for t in range(NT):
-            ps = psum4.tile([P, S], F32, name="dd")
-            mm(ps[:], key_w[:, blk(t)], key_sc[:, blk(t)], bw[:], bsc[:])
-            if t < 1:
-                nc.scalar.copy(b_sb[t][:], ps[:])
+            mm(b_ps[t][:], key_w[:, blk(t)], key_sc[:, blk(t)], bw[:], bsc[:])
+        for t in range(NT):
+            mm(a_ps[t][:], key_w[:, blk(t)], key_sc[:, blk(t)], aw[:], asc[:])
+        nc.scalar.copy(b_sb[:, 0, :], b_ps[0][:])
+        for t in range(1, NT):
+            nc.vector.tensor_copy(b_sb[:, t, :], b_ps[t][:])
+
+        def pr(u):
+            return slice(2 * u, 2 * u + 2)
+
+        def a_out(t):
+            if t != 2:
+                nc.vector.tensor_scalar(a_sb[:, t, :], a_ps[t][:], g16[:, t : t + 1], None, ALU.mult)
             else:
-                nc.vector.tensor_copy(b_sb[t][:], ps[:])
+                nc.scalar.activation(out=a_sb[:, t, :], in_=a_ps[t][:], func=ACT.Copy, scale=g16[:, t : t + 1])
+
+        def fetch_b(buf, t, lo):
+            gather(buf[:, t % 2, :], b_sb[:, t, :], n2_t, lo, lo + HALF, 1.0)
+
+        def fetch_a(buf, t, lo, hi):
+            gather(buf[:, t % 2, lo % HALF : lo % HALF + hi - lo], a_sb[:, t, :], n1_t, lo, hi, 0.5)
+
+        def squash(dst, u, lo):
+            nc.scalar.activation(out=dst[:], in_=dif[:, pr(u), lo : lo + HALF], func=ACT.Tanh, scale=0.03125)
+
+        def half_pull(buf, u, lo, hi):
+            o = lo % HALF
+            nc.vector.scalar_tensor_tensor(pull[:, pr(u), lo:hi], a_sb[:, pr(u), lo:hi], -0.5, buf[:, :, o : o + hi - lo], ALU.mult, ALU.add)
+
+        def weigh(th, u, lo, hi):
+            o = lo % HALF
+            nc.vector.scalar_tensor_tensor(step[:, pr(u), lo:hi], th[:, :, o : o + hi - lo], 1.0, pull[:, pr(u), lo:hi], ALU.add, ALU.mult)
+
+        def blend(lo, hi):
+            nc.vector.tensor_tensor(
+                z_bf[:, lo:hi, :].rearrange("p (c i) t -> p c t i", i=4),
+                step[:, :, lo:hi].rearrange("p t (c i) -> p c t i", i=4),
+                a_sb[:, :, lo:hi].rearrange("p t (c i) -> p c t i", i=4),
+                ALU.add,
+            )
+
+        def close(lo, hi):
+            nc.vector.quantize_mx(out=z_q[:, lo:hi].bitcast(FP8X4), scales=z_s[:, lo:hi], in_=z_bf[:, lo:hi, :].rearrange("p j t -> p (j t)"))
+            for t in range(NT):
+                mm(hbank[t][:, lo:hi], w_q[:, blk(t)], w_s[:, blk(t)], z_q[:, lo:hi], z_s[:, lo:hi])
+
+        def first_out(lo, hi):
+            nc.scalar.copy(h_sb[0][:, lo:hi], hbank[0][:, lo:hi])
+
+        def differ_ps(buf, t):
+            nc.vector.tensor_tensor(dif[:, t, 0:HALF], buf[:, t % 2, :], b_ps[t][:, 0:HALF], ALU.subtract)
+
+        bg0 = [pair_buffer("got", u) for u in range(2)]
         for t in range(NT):
-            ps = psum.tile([P, S], F32, name="zz") if t < 2 else psum1.tile([P, S], F32, name=("ee", "aa")[t - 2])
-            mm(ps[:], key_w[:, blk(t)], key_sc[:, blk(t)], aw[:], asc[:])
-            nc.vector.tensor_scalar(a_sb[:, t, :], ps[:], gain[:, t : t + 1], 0.0625, ALU.mult, ALU.mult)
+            fetch_b(bg0[t // 2], t, 0)
+        a_out(0)
+        differ_ps(bg0[0], 0)
+        differ_ps(bg0[0], 1)
+        a_out(1)
+        differ_ps(bg0[1], 2)
+        differ_ps(bg0[1], 3)
+        a_out(3)
+        a_out(2)
+        hbank = [psum4.tile([P, S], F32, name="bh") for t in range(NT)]
+        ag0 = [pair_buffer("got", u) for u in range(2)]
+        th0 = [pair_buffer("th", u) for u in range(2)]
+        fetch_a(ag0[0], 0, 0, HALF)
+        squash(th0[0], 0, 0)
+        fetch_a(ag0[0], 1, 0, HALF)
+        squash(th0[1], 1, 0)
+        fetch_a(ag0[1], 2, 0, HALF)
+        fetch_a(ag0[1], 3, 0, HALF)
         nc.vector.quantize_mx(out=w_q[:].bitcast(FP8X4), scales=w_s[:], in_=w_bf[:].rearrange("p t m j -> p (t m j)"))
-
-        dbank = [psum4.tile([P, NT, P], F32, name="dd") for jb in range(NT)]
+        half_pull(ag0[0], 0, 0, HALF)
+        weigh(th0[0], 0, 0, HALF)
+        half_pull(ag0[1], 1, 0, HALF)
+        bg1 = [pair_buffer("got", u) for u in range(2)]
         for t in range(NT):
-            for lo, hi in CHUNKS:
-                gather_neg(bg[:, t, :], b_sb[t][:], n2_t, lo, hi)
-                for jb in range(lo // P, hi // P):
-                    diff_t(dbank[jb], b_sb[t], bg[:, t, :], t, jb)
-        sg = [keep.tile([P, NT, P], F32, name="sg%d" % jb) for jb in range(NT)]
-        ebank = {}
-        zb = {}
-        hbank = []
-
-        def pull(jb):
-            ebank[jb] = psum1.tile([P, NT, P], F32, name="ee")
-            for t in range(NT):
-                gather_neg(ag[:, t, :], a_sb[:, t, :], n1_t, jb * P, (jb + 1) * P)
-                diff_t(ebank[jb], a_sb[:, t, :], ag[:, t, :], t, jb)
-
-        def gate(jb):
-            nc.scalar.activation(out=sg[jb][:], in_=dbank[jb][:], func=ACT.Sigmoid, scale=-0.0625)
-
-        def weigh(jb):
-            mt = work.tile([P, NT, P], F32, name="mt")
-            nc.vector.tensor_tensor(mt[:], ebank[jb][:], sg[jb][:], ALU.mult)
-            zb[jb] = psum.tile([P, NT, P], F32, name="zz")
-            for t in range(NT):
-                nc.tensor.transpose(zb[jb][:, t, :], mt[:, t, :], ident[:])
-
-        def finish(jb):
-            zf = work.tile([P, P, NT], BF16, name="zf", align_bytes=64)
-            nc.vector.tensor_tensor(zf[:], a_sb[:, :, blk(jb)].rearrange("p t j -> p j t"), zb[jb][:].rearrange("p t j -> p j t"), ALU.subtract)
-            nc.vector.quantize_mx(out=z_q[:, blk(jb)].bitcast(FP8X4), scales=z_s[:, blk(jb)], in_=zf[:].rearrange("p j t -> p (j t)"))
-            for t in range(NT):
-                mm(hbank[t][:, blk(jb)], w_q[:, blk(t)], w_s[:, blk(t)], z_q[:, blk(jb)], z_s[:, blk(jb)])
-
-        pull(0)
-        gate(0)
-        gate(1)
-        weigh(0)
-        pull(1)
-        gate(2)
-        gate(3)
-        hbank.extend(psum4.tile([P, S], F32, name="dd") for t in range(NT))
-        finish(0)
-        weigh(1)
-        pull(2)
-        finish(1)
-        weigh(2)
-        pull(3)
-        finish(2)
-        nc.vector.tensor_copy(h_sb[0][:, 0:384], hbank[0][:, 0:384])
-        weigh(3)
-        finish(3)
-        nc.vector.tensor_copy(h_sb[0][:, 384:512], hbank[0][:, 384:512])
+            fetch_b(bg1[t // 2], t, HALF)
+        weigh(th0[1], 1, 0, HALF)
+        nc.vector.tensor_tensor(dif[:, pr(0), HALF:S], bg1[0][:], b_sb[:, pr(0), HALF:S], ALU.subtract)
+        blend(0, HALF)
+        nc.vector.tensor_tensor(dif[:, pr(1), HALF:S], bg1[1][:], b_sb[:, pr(1), HALF:S], ALU.subtract)
+        close(0, HALF)
+        ag1 = [pair_buffer("th", u) for u in range(2)]
+        th1 = [pair_buffer("got", u) for u in range(2)]
+        for u in range(2):
+            fetch_a(ag1[u], 2 * u, 256, 384)
+            fetch_a(ag1[u], 2 * u + 1, 256, 384)
+            squash(th1[u], u, HALF)
+        for t in range(NT):
+            fetch_a(ag1[t // 2], t, 384, 512)
+        half_pull(ag1[0], 0, 256, 384)
+        half_pull(ag1[1], 1, 256, 384)
+        weigh(th1[0], 0, 256, 384)
+        weigh(th1[1], 1, 256, 384)
+        blend(256, 384)
+        half_pull(ag1[0], 0, 384, 512)
+        close(256, 384)
+        weigh(th1[0], 0, 384, 512)
+        half_pull(ag1[1], 1, 384, 512)
+        weigh(th1[1], 1, 384, 512)
+        first_out(0, 256)
+        blend(384, 512)
+        close(384, 512)
+        first_out(256, 384)
+        first_out(384, 512)
 
         rows = out.rearrange("(p t) j -> p t j", t=NT)
         for t in range(NT):

@@ -41,14 +41,12 @@ def tile_picked_twkspullbbig_none_p_kernel(tc, x_words, x_scales, d_words, d_sca
 
         k1_t = load_list(k1, "k1_t")
         two_t = load_list(two, "two_t")
-        offs_t = load_list(offs, "offs_t")
-        nc.scalar.dma_start(dsc[0:P:8, :].bitcast(I32), d_scales[0].bitcast(I32))
+        nc.sync.dma_start(dsc[0:P:8, :].bitcast(I32), d_scales[0].bitcast(I32))
         for q in range(4):
             nc.scalar.dma_start(xsc[32 * q : 32 * q + 4, :].bitcast(I32), x_scales[0, 4 * q : 4 * q + 4, :].bitcast(I32))
         nc.sync.dma_start(dw[:].bitcast(I32), d_words[0].rearrange("p n t -> p (n t)").bitcast(I32))
         nc.sync.dma_start(xw[:].bitcast(I32), x_words[0].rearrange("p n t -> p (n t)").bitcast(I32))
-        w_raw = keep.tile([P, 4, S], F32, name="w_raw")
-        nc.sync.dma_start(w_raw[:], w1.rearrange("(p j) c -> p j c", j=4))
+        offs_t = load_list(offs, "offs_t")
         n2_t = load_list(n2, "n2_t")
         gain = keep.tile([P, NT], F32, name="gain")
         nc.sync.dma_start(gain[:], gn.rearrange("(p t) o -> p (t o)", t=NT))
@@ -62,18 +60,16 @@ def tile_picked_twkspullbbig_none_p_kernel(tc, x_words, x_scales, d_words, d_sca
         for j in range(1, 4):
             nc.scalar.dma_start(key_sc[j:P:32, :].bitcast(I32), key_sc[8 * j : P : 32, :].bitcast(I32))
 
+        w_raw = keep.tile([P, 4, S], F32, name="ksc_g", align_bytes=64)
+        nc.scalar.dma_start(w_raw[:], w1.rearrange("(p j) c -> p j c", j=4))
         bsc = keep.tile([P, S], U8, name="bsc", align_bytes=64)
         nc.vector.tensor_copy(bsc[:], xsc[:].indirect(two_t[:]))
         kw_g = keep.tile([P, S], U32, name="kw_g", align_bytes=64)
         nc.vector.tensor_copy(kw_g[:], dw[:].indirect(k1_t[:]))
         key_w = keep.tile([P, S], U32, name="key_w", align_bytes=64)
         nc.vector.tensor_copy(key_w[:].rearrange("p (t a b) -> p a t b", t=NT, b=4), kw_g[:].rearrange("p (a b t) -> p a t b", t=NT, b=4))
-        asc = keep.tile([P, S], U8, name="asc", align_bytes=64)
-        nc.vector.tensor_copy(asc[:], xsc[:].indirect(offs_t[:]))
         bw = keep.tile([P, S], U32, name="bw", align_bytes=64)
         nc.vector.tensor_copy(bw[:], xw[:].indirect(two_t[:]))
-        aw = keep.tile([P, S], U32, name="aw", align_bytes=64)
-        nc.vector.tensor_copy(aw[:], xw[:].indirect(offs_t[:]))
 
         def blk(i):
             return slice(i * P, (i + 1) * P)
@@ -81,140 +77,135 @@ def tile_picked_twkspullbbig_none_p_kernel(tc, x_words, x_scales, d_words, d_sca
         def mm(dst, lw, ls, rw, rs):
             nc.tensor.matmul_mx(out=dst, lhsT=lw.bitcast(FP8X4), lhsT_scale=ls, rhs=rw.bitcast(FP8X4), rhs_scale=rs, start=True, stop=True)
 
-        w_bf = keep.tile([P, NT, P, 4], BF16, name="w_bf", align_bytes=64)
-        for t in range(NT):
-            nc.gpsimd.tensor_copy(w_bf[:, t, :, :], w_raw[:].rearrange("p j (m t) -> p t m j", t=NT)[:, t, :, :])
         w_q = keep.tile([P, S], U32, name="w_q", align_bytes=64)
         w_s = keep.tile([P, S], U8, name="w_s", align_bytes=64)
 
-        b_sb = keep.tile([P, NT, S], F32, name="b_sb")
-        a_sb = keep.tile([P, NT, S], F32, name="a_sb")
-        dif = keep.tile([P, NT, S], F32, name="dif")
-        pull = keep.tile([P, NT, S], F32, name="pull")
-        step = keep.tile([P, NT, S], F32, name="step")
+        b_sb = [keep.tile([P, S], F32, name="b_sb%d" % t) for t in range(NT)]
+        a_sb = [keep.tile([P, S], F32, name="a_sb%d" % t) for t in range(NT)]
+        th = keep.tile([P, NT, S], F32, name="th")
+        stay = keep.tile([P, NT, S], F32, name="stay")
+        move = keep.tile([P, NT, S], F32, name="move")
         z_bf = keep.tile([P, S, NT], BF16, name="z_bf", align_bytes=64)
         z_q = keep.tile([P, S], U32, name="z_q", align_bytes=64)
         z_s = keep.tile([P, S], U8, name="z_s", align_bytes=64)
         h_sb = [keep.tile([P, S], F32, name="h_sb%d" % t) for t in range(NT)]
-        g16 = keep.tile([P, NT], F32, name="g16")
-        nc.gpsimd.tensor_scalar(g16[:], gain[:], 0.0625, 0.0, ALU.mult, ALU.add)
+        g32 = keep.tile([P, NT], F32, name="g32")
+        nc.gpsimd.tensor_scalar(g32[:], gain[:], 0.03125, 0.0, ALU.mult, ALU.add)
 
-        def pair_buffer(tag, u):
-            return keep.tile([P, 2, HALF], F32, name="%s%d" % (tag, u))
-
-        def gather(dst, window, lst, lo, hi, scale):
-            nc.scalar.activation(out=dst, in_=window.indirect(lst[:, lo // 16 : hi // 16]), func=ACT.Copy, scale=scale)
+        def gather(dst, window, lst, lo, hi):
+            nc.scalar.activation(out=dst, in_=window[:].indirect(lst[:, lo // 16 : hi // 16]), func=ACT.Copy)
 
         b_ps = [psum4.tile([P, S], F32, name="bh") for t in range(NT)]
         a_ps = [psum4.tile([P, S], F32, name="aa") for t in range(NT)]
         for t in range(NT):
             mm(b_ps[t][:], key_w[:, blk(t)], key_sc[:, blk(t)], bw[:], bsc[:])
+        asc = keep.tile([P, S], U8, name="kw_g", align_bytes=64)
+        nc.vector.tensor_copy(asc[:], xsc[:].indirect(offs_t[:]))
+        aw = keep.tile([P, S], U32, name="aw", align_bytes=64)
+        nc.vector.tensor_copy(aw[:], xw[:].indirect(offs_t[:]))
         for t in range(NT):
             mm(a_ps[t][:], key_w[:, blk(t)], key_sc[:, blk(t)], aw[:], asc[:])
-        nc.scalar.copy(b_sb[:, 0, :], b_ps[0][:])
-        for t in range(1, NT):
-            nc.vector.tensor_copy(b_sb[:, t, :], b_ps[t][:])
+        w_bf = keep.tile([P, NT, P, 4], BF16, name="xw", align_bytes=64)
+        for t in range(NT):
+            nc.gpsimd.tensor_copy(w_bf[:, t, :, :], w_raw[:].rearrange("p j (m t) -> p t m j", t=NT)[:, t, :, :])
+        for t in range(2):
+            nc.scalar.copy(b_sb[t][:], b_ps[t][:])
+        for t in range(2, NT):
+            nc.vector.tensor_copy(b_sb[t][:], b_ps[t][:])
 
         def pr(u):
             return slice(2 * u, 2 * u + 2)
 
+        bg = {}
+        dif = {}
+
+        def fetch_b(t):
+            bg[t] = keep.tile([P, S], F32, name="dif0" if t == 3 else "bg%d" % t)
+            for lo in (0, HALF):
+                gather(bg[t][:, lo : lo + HALF], b_sb[t], n2_t, lo, lo + HALF)
+
         def a_out(t):
-            if t != 2:
-                nc.vector.tensor_scalar(a_sb[:, t, :], a_ps[t][:], g16[:, t : t + 1], None, ALU.mult)
-            else:
-                nc.scalar.activation(out=a_sb[:, t, :], in_=a_ps[t][:], func=ACT.Copy, scale=g16[:, t : t + 1])
+            nc.vector.tensor_scalar(a_sb[t][:], a_ps[t][:], g32[:, t : t + 1], None, ALU.mult)
 
-        def fetch_b(buf, t, lo):
-            gather(buf[:, t % 2, :], b_sb[:, t, :], n2_t, lo, lo + HALF, 1.0)
+        def differ(t):
+            dif[t] = keep.tile([P, S], F32, name="dif%d" % t)
+            nc.vector.tensor_tensor(dif[t][:], bg[t][:], b_ps[t][:], ALU.subtract)
 
-        def fetch_a(buf, t, lo, hi):
-            gather(buf[:, t % 2, lo % HALF : lo % HALF + hi - lo], a_sb[:, t, :], n1_t, lo, hi, 0.5)
+        def squash(t):
+            nc.scalar.activation(out=th[:, t, :], in_=dif[t][:], func=ACT.Tanh, scale=0.03125)
 
-        def squash(dst, u, lo):
-            nc.scalar.activation(out=dst[:], in_=dif[:, pr(u), lo : lo + HALF], func=ACT.Tanh, scale=0.03125)
+        def own_share(t):
+            nc.vector.scalar_tensor_tensor(stay[:, t, :], th[:, t, :], 1.0, a_sb[t][:], ALU.subtract, ALU.mult)
 
-        def half_pull(buf, u, lo, hi):
-            o = lo % HALF
-            nc.vector.scalar_tensor_tensor(pull[:, pr(u), lo:hi], a_sb[:, pr(u), lo:hi], -0.5, buf[:, :, o : o + hi - lo], ALU.mult, ALU.add)
+        fetch_b(0)
+        fetch_b(1)
+        a_out(0)
+        differ(0)
+        a_out(1)
+        differ(1)
+        fetch_b(2)
+        squash(0)
+        fetch_b(3)
+        a_out(2)
+        differ(2)
+        squash(1)
+        a_out(3)
+        own_share(0)
+        differ(3)
+        squash(2)
+        ag_first = keep.tile([P, 2, P], F32, name="dif2")
+        for t in range(2):
+            gather(ag_first[:, t, :], a_sb[t], n1_t, 0, P)
+        squash(3)
+        ag = keep.tile([P, NT, S], F32, name="dif3")
 
-        def weigh(th, u, lo, hi):
-            o = lo % HALF
-            nc.vector.scalar_tensor_tensor(step[:, pr(u), lo:hi], th[:, :, o : o + hi - lo], 1.0, pull[:, pr(u), lo:hi], ALU.add, ALU.mult)
+        def fetch_a(t, cols):
+            gather(ag[:, t, cols], a_sb[t], n1_t, cols.start, cols.stop)
 
-        def blend(lo, hi):
+        def other_share(tiles, cols, src):
+            nc.vector.scalar_tensor_tensor(move[:, tiles, cols], th[:, tiles, cols], 1.0, src, ALU.add, ALU.mult)
+
+        def blend(cols):
             nc.vector.tensor_tensor(
-                z_bf[:, lo:hi, :].rearrange("p (c i) t -> p c t i", i=4),
-                step[:, :, lo:hi].rearrange("p t (c i) -> p c t i", i=4),
-                a_sb[:, :, lo:hi].rearrange("p t (c i) -> p c t i", i=4),
-                ALU.add,
+                z_bf[:, cols, :].rearrange("p (c i) t -> p c t i", i=4),
+                move[:, :, cols].rearrange("p t (c i) -> p c t i", i=4),
+                stay[:, :, cols].rearrange("p t (c i) -> p c t i", i=4),
+                ALU.subtract,
             )
 
-        def close(lo, hi):
-            nc.vector.quantize_mx(out=z_q[:, lo:hi].bitcast(FP8X4), scales=z_s[:, lo:hi], in_=z_bf[:, lo:hi, :].rearrange("p j t -> p (j t)"))
+        def close(cols):
+            nc.vector.quantize_mx(out=z_q[:, cols].bitcast(FP8X4), scales=z_s[:, cols], in_=z_bf[:, cols, :].rearrange("p j t -> p (j t)"))
             for t in range(NT):
-                mm(hbank[t][:, lo:hi], w_q[:, blk(t)], w_s[:, blk(t)], z_q[:, lo:hi], z_s[:, lo:hi])
+                dst = hlast if (t == 0 and cols.stop == S) else hbank[t]
+                mm(dst[:, cols], w_q[:, blk(t)], w_s[:, blk(t)], z_q[:, cols], z_s[:, cols])
 
-        def first_out(lo, hi):
-            nc.scalar.copy(h_sb[0][:, lo:hi], hbank[0][:, lo:hi])
-
-        def differ_ps(buf, t):
-            nc.vector.tensor_tensor(dif[:, t, 0:HALF], buf[:, t % 2, :], b_ps[t][:, 0:HALF], ALU.subtract)
-
-        bg0 = [pair_buffer("got", u) for u in range(2)]
-        for t in range(NT):
-            fetch_b(bg0[t // 2], t, 0)
-        a_out(0)
-        differ_ps(bg0[0], 0)
-        differ_ps(bg0[0], 1)
-        a_out(1)
-        differ_ps(bg0[1], 2)
-        differ_ps(bg0[1], 3)
-        a_out(3)
-        a_out(2)
         hbank = [psum4.tile([P, S], F32, name="bh") for t in range(NT)]
-        ag0 = [pair_buffer("got", u) for u in range(2)]
-        th0 = [pair_buffer("th", u) for u in range(2)]
-        fetch_a(ag0[0], 0, 0, HALF)
-        squash(th0[0], 0, 0)
-        fetch_a(ag0[0], 1, 0, HALF)
-        squash(th0[1], 1, 0)
-        fetch_a(ag0[1], 2, 0, HALF)
-        fetch_a(ag0[1], 3, 0, HALF)
+        hlast = psum4.tile([P, S], F32, name="aa")
+        head, body, tail = slice(0, 128), slice(128, 384), slice(384, 512)
+        fetch_a(2, head)
+        fetch_a(3, head)
+        own_share(1)
         nc.vector.quantize_mx(out=w_q[:].bitcast(FP8X4), scales=w_s[:], in_=w_bf[:].rearrange("p t m j -> p (t m j)"))
-        half_pull(ag0[0], 0, 0, HALF)
-        weigh(th0[0], 0, 0, HALF)
-        half_pull(ag0[1], 1, 0, HALF)
-        bg1 = [pair_buffer("got", u) for u in range(2)]
+        own_share(2)
+        other_share(pr(0), head, ag_first[:])
+        own_share(3)
+        other_share(pr(1), head, ag[:, pr(1), head])
         for t in range(NT):
-            fetch_b(bg1[t // 2], t, HALF)
-        weigh(th0[1], 1, 0, HALF)
-        nc.vector.tensor_tensor(dif[:, pr(0), HALF:S], bg1[0][:], b_sb[:, pr(0), HALF:S], ALU.subtract)
-        blend(0, HALF)
-        nc.vector.tensor_tensor(dif[:, pr(1), HALF:S], bg1[1][:], b_sb[:, pr(1), HALF:S], ALU.subtract)
-        close(0, HALF)
-        ag1 = [pair_buffer("th", u) for u in range(2)]
-        th1 = [pair_buffer("got", u) for u in range(2)]
-        for u in range(2):
-            fetch_a(ag1[u], 2 * u, 256, 384)
-            fetch_a(ag1[u], 2 * u + 1, 256, 384)
-            squash(th1[u], u, HALF)
+            fetch_a(t, body)
+        blend(head)
+        other_share(pr(0), body, ag[:, pr(0), body])
+        close(head)
+        other_share(pr(1), body, ag[:, pr(1), body])
         for t in range(NT):
-            fetch_a(ag1[t // 2], t, 384, 512)
-        half_pull(ag1[0], 0, 256, 384)
-        half_pull(ag1[1], 1, 256, 384)
-        weigh(th1[0], 0, 256, 384)
-        weigh(th1[1], 1, 256, 384)
-        blend(256, 384)
-        half_pull(ag1[0], 0, 384, 512)
-        close(256, 384)
-        weigh(th1[0], 0, 384, 512)
-        half_pull(ag1[1], 1, 384, 512)
-        weigh(th1[1], 1, 384, 512)
-        first_out(0, 256)
-        blend(384, 512)
-        close(384, 512)
-        first_out(256, 384)
-        first_out(384, 512)
+            fetch_a(t, tail)
+        blend(body)
+        other_share(pr(0), tail, ag[:, pr(0), tail])
+        close(body)
+        other_share(pr(1), tail, ag[:, pr(1), tail])
+        blend(tail)
+        close(tail)
+        nc.scalar.copy(h_sb[0][:, 0:384], hbank[0][:, 0:384])
+        nc.scalar.copy(h_sb[0][:, 384:S], hlast[:, 384:S])
 
         rows = out.rearrange("(p t) j -> p t j", t=NT)
         for t in range(NT):

@@ -1,6 +1,7 @@
 from contextlib import ExitStack
 
 import concourse.mybir as mybir
+from concourse.masks import make_identity
 
 F32 = mybir.dt.float32
 BF16 = mybir.dt.bfloat16
@@ -62,10 +63,10 @@ def tile_picked_twkspullbbig_none_p_kernel(tc, x_words, x_scales, d_words, d_sca
 
         w_raw = keep.tile([P, 4, S], F32, name="ksc_g", align_bytes=64)
         nc.scalar.dma_start(w_raw[:], w1.rearrange("(p j) c -> p j c", j=4))
-        bsc = keep.tile([P, S], U8, name="bsc", align_bytes=64)
-        nc.vector.tensor_copy(bsc[:], xsc[:].indirect(two_t[:]))
         kw_g = keep.tile([P, S], U32, name="kw_g", align_bytes=64)
         nc.vector.tensor_copy(kw_g[:], dw[:].indirect(k1_t[:]))
+        bsc = keep.tile([P, S], U8, name="dw", align_bytes=64)
+        nc.vector.tensor_copy(bsc[:], xsc[:].indirect(two_t[:]))
         key_w = keep.tile([P, S], U32, name="key_w", align_bytes=64)
         nc.vector.tensor_copy(key_w[:].rearrange("p (t a b) -> p a t b", t=NT, b=4), kw_g[:].rearrange("p (a b t) -> p a t b", t=NT, b=4))
         bw = keep.tile([P, S], U32, name="bw", align_bytes=64)
@@ -82,7 +83,6 @@ def tile_picked_twkspullbbig_none_p_kernel(tc, x_words, x_scales, d_words, d_sca
 
         b_sb = [keep.tile([P, S], F32, name="b_sb%d" % t) for t in range(NT)]
         a_sb = [keep.tile([P, S], F32, name="a_sb%d" % t) for t in range(NT)]
-        th = keep.tile([P, NT, S], F32, name="th")
         stay = keep.tile([P, NT, S], F32, name="stay")
         move = keep.tile([P, NT, S], F32, name="move")
         z_bf = keep.tile([P, S, NT], BF16, name="z_bf", align_bytes=64)
@@ -92,8 +92,8 @@ def tile_picked_twkspullbbig_none_p_kernel(tc, x_words, x_scales, d_words, d_sca
         g32 = keep.tile([P, NT], F32, name="g32")
         nc.gpsimd.tensor_scalar(g32[:], gain[:], 0.03125, 0.0, ALU.mult, ALU.add)
 
-        def gather(dst, window, lst, lo, hi):
-            nc.scalar.activation(out=dst, in_=window[:].indirect(lst[:, lo // 16 : hi // 16]), func=ACT.Copy)
+        def gather(dst, window, lst, lo, hi, scale=1.0):
+            nc.scalar.activation(out=dst, in_=window[:].indirect(lst[:, lo // 16 : hi // 16]), func=ACT.Copy, scale=scale)
 
         b_ps = [psum4.tile([P, S], F32, name="bh") for t in range(NT)]
         a_ps = [psum4.tile([P, S], F32, name="aa") for t in range(NT)]
@@ -105,65 +105,49 @@ def tile_picked_twkspullbbig_none_p_kernel(tc, x_words, x_scales, d_words, d_sca
         nc.vector.tensor_copy(aw[:], xw[:].indirect(offs_t[:]))
         for t in range(NT):
             mm(a_ps[t][:], key_w[:, blk(t)], key_sc[:, blk(t)], aw[:], asc[:])
-        w_bf = keep.tile([P, NT, P, 4], BF16, name="xw", align_bytes=64)
+        ident_t = keep.tile([P, P], F32, name="xw", align_bytes=64)
+        ident = ident_t[:]
+        make_identity(nc, ident)
+        w_bf_t = keep.tile([P, NT * S], BF16, name="dw", align_bytes=64)
+        w_bf = w_bf_t[:]
         for t in range(NT):
-            nc.gpsimd.tensor_copy(w_bf[:, t, :, :], w_raw[:].rearrange("p j (m t) -> p t m j", t=NT)[:, t, :, :])
-        for t in range(2):
-            nc.scalar.copy(b_sb[t][:], b_ps[t][:])
-        for t in range(2, NT):
+            nc.gpsimd.tensor_copy(
+                w_bf[:, t * S : (t + 1) * S].rearrange("p (g e j) -> p g e j", e=16, j=4),
+                w_raw[:].rearrange("p j (g t e) -> p t g e j", t=NT, e=16)[:, t],
+            )
+        nc.scalar.copy(b_sb[0][:], b_ps[0][:])
+        for t in range(1, NT):
             nc.vector.tensor_copy(b_sb[t][:], b_ps[t][:])
-
-        def pr(u):
-            return slice(2 * u, 2 * u + 2)
-
-        bg = {}
-        dif = {}
-
-        def fetch_b(t):
-            bg[t] = keep.tile([P, S], F32, name="dif0" if t == 3 else "bg%d" % t)
-            for lo in (0, HALF):
-                gather(bg[t][:, lo : lo + HALF], b_sb[t], n2_t, lo, lo + HALF)
-
-        def a_out(t):
+        for t in range(NT):
             nc.vector.tensor_scalar(a_sb[t][:], a_ps[t][:], g32[:, t : t + 1], None, ALU.mult)
 
-        def differ(t):
-            dif[t] = keep.tile([P, S], F32, name="dif%d" % t)
-            nc.vector.tensor_tensor(dif[t][:], bg[t][:], b_ps[t][:], ALU.subtract)
+        bg = [keep.tile([P, S], F32, name="bg%d" % t) for t in range(NT)]
+        dif = [psum4.tile([P, NT, P], F32, name="bh") for t in range(NT)]
+        for t in range(NT):
+            for lo in (0, HALF):
+                gather(bg[t][:, lo : lo + HALF], b_sb[t], n2_t, lo, lo + HALF, -1.0)
+            for c in range(NT):
+                nc.tensor.matmul(dif[t][:, c, :], b_sb[t][:, blk(c)], ident, start=True, stop=False, is_transpose=True)
+                nc.tensor.matmul(dif[t][:, c, :], bg[t][:, blk(c)], ident, start=False, stop=True, is_transpose=True)
+
+        ag3 = keep.tile([P, S], F32, name="ag3")
+        for lo in (0, HALF):
+            nc.vector.tensor_copy(ag3[:, lo : lo + HALF], a_sb[3][:].indirect(n1_t[:, lo // 16 : (lo + HALF) // 16]))
+        nc.vector.quantize_mx(out=w_q[:].bitcast(FP8X4), scales=w_s[:], in_=w_bf)
+
+        th = [psum4.tile([P, S], F32, name="aa") for t in range(NT)]
 
         def squash(t):
-            nc.scalar.activation(out=th[:, t, :], in_=dif[t][:], func=ACT.Tanh, scale=0.03125)
+            turned = keep.tile([P, NT, P], F32, name="turned%d" % t)
+            nc.scalar.activation(out=turned[:], in_=dif[t][:], func=ACT.Tanh, scale=-0.03125)
+            for c in range(NT):
+                nc.tensor.transpose(th[t][:, blk(c)], turned[:, c, :], ident)
 
         def own_share(t):
-            nc.vector.scalar_tensor_tensor(stay[:, t, :], th[:, t, :], 1.0, a_sb[t][:], ALU.subtract, ALU.mult)
+            nc.vector.scalar_tensor_tensor(stay[:, t, :], th[t][:], 1.0, a_sb[t][:], ALU.subtract, ALU.mult)
 
-        fetch_b(0)
-        fetch_b(1)
-        a_out(0)
-        differ(0)
-        a_out(1)
-        differ(1)
-        fetch_b(2)
-        squash(0)
-        fetch_b(3)
-        a_out(2)
-        differ(2)
-        squash(1)
-        a_out(3)
-        own_share(0)
-        differ(3)
-        squash(2)
-        ag_first = keep.tile([P, 2, P], F32, name="dif2")
-        for t in range(2):
-            gather(ag_first[:, t, :], a_sb[t], n1_t, 0, P)
-        squash(3)
-        ag = keep.tile([P, NT, S], F32, name="dif3")
-
-        def fetch_a(t, cols):
-            gather(ag[:, t, cols], a_sb[t], n1_t, cols.start, cols.stop)
-
-        def other_share(tiles, cols, src):
-            nc.vector.scalar_tensor_tensor(move[:, tiles, cols], th[:, tiles, cols], 1.0, src, ALU.add, ALU.mult)
+        def other_share(t, cols, src):
+            nc.vector.scalar_tensor_tensor(move[:, t, cols], th[t][:, cols], 1.0, src, ALU.add, ALU.mult)
 
         def blend(cols):
             nc.vector.tensor_tensor(
@@ -179,41 +163,54 @@ def tile_picked_twkspullbbig_none_p_kernel(tc, x_words, x_scales, d_words, d_sca
                 dst = hlast if (t == 0 and cols.stop == S) else hbank[t]
                 mm(dst[:, cols], w_q[:, blk(t)], w_s[:, blk(t)], z_q[:, cols], z_s[:, cols])
 
+        head, body, tail = slice(0, 128), slice(128, 384), slice(384, 512)
+        for t in range(3):
+            squash(t)
+        ag_first = keep.tile([P, 2, P], F32, name="bg2")
+        for t in range(2):
+            gather(ag_first[:, t, :], a_sb[t], n1_t, 0, P)
+        squash(3)
+        ag = keep.tile([P, 3, S], F32, name="bg3")
+
+        def fetch_a(t, cols):
+            gather(ag[:, t, cols], a_sb[t], n1_t, cols.start, cols.stop)
+
         hbank = [psum4.tile([P, S], F32, name="bh") for t in range(NT)]
         hlast = psum4.tile([P, S], F32, name="aa")
-        head, body, tail = slice(0, 128), slice(128, 384), slice(384, 512)
         fetch_a(2, head)
-        fetch_a(3, head)
+        for cols in (body, tail):
+            for t in range(3):
+                fetch_a(t, cols)
+        own_share(0)
         own_share(1)
-        nc.vector.quantize_mx(out=w_q[:].bitcast(FP8X4), scales=w_s[:], in_=w_bf[:].rearrange("p t m j -> p (t m j)"))
+        other_share(0, head, ag_first[:, 0, :])
+        other_share(1, head, ag_first[:, 1, :])
         own_share(2)
-        other_share(pr(0), head, ag_first[:])
+        other_share(2, head, ag[:, 2, head])
         own_share(3)
-        other_share(pr(1), head, ag[:, pr(1), head])
-        for t in range(NT):
-            fetch_a(t, body)
+        other_share(3, slice(0, S), ag3[:])
         blend(head)
-        other_share(pr(0), body, ag[:, pr(0), body])
+        other_share(0, body, ag[:, 0, body])
         close(head)
-        other_share(pr(1), body, ag[:, pr(1), body])
-        for t in range(NT):
-            fetch_a(t, tail)
+        other_share(1, body, ag[:, 1, body])
+        other_share(2, body, ag[:, 2, body])
         blend(body)
-        other_share(pr(0), tail, ag[:, pr(0), tail])
+        other_share(0, tail, ag[:, 0, tail])
+        other_share(1, tail, ag[:, 1, tail])
         close(body)
-        other_share(pr(1), tail, ag[:, pr(1), tail])
+        other_share(2, tail, ag[:, 2, tail])
         blend(tail)
         close(tail)
         nc.scalar.copy(h_sb[0][:, 0:384], hbank[0][:, 0:384])
         nc.scalar.copy(h_sb[0][:, 384:S], hlast[:, 384:S])
 
-        rows = out.rearrange("(p t) j -> p t j", t=NT)
+        rows = out.rearrange("(g t e) j -> t g e j", t=NT, e=16)
         for t in range(NT):
             if t + 1 < NT:
                 nc.vector.tensor_copy(h_sb[t + 1][:], hbank[t + 1][:])
             hg = keep.tile([P, S], F32, name="hg%d" % t)
             res = keep.tile([P, S], F32, name="res%d" % t)
-            for lo, hi in ((0, 256), (256, 512)):
+            for lo, hi in ((0, 256), (256, 512)) if t + 1 < NT else ((0, 256), (256, 384), (384, 512)):
                 nc.scalar.activation(out=hg[:, lo:hi], in_=h_sb[t][:].indirect(n3_t[:, lo // 16 : hi // 16]), func=ACT.Copy)
                 nc.vector.tensor_tensor(res[:, lo:hi], hg[:, lo:hi], h_sb[t][:, lo:hi], ALU.max)
-                nc.sync.dma_start(rows[:, t, lo:hi], res[:, lo:hi])
+                nc.sync.dma_start(rows[t][:, :, lo:hi], res[:, lo:hi])

from contextlib import ExitStack

import concourse.mybir as mybir
from concourse.masks import make_identity

F32 = mybir.dt.float32
BF16 = mybir.dt.bfloat16
I32 = mybir.dt.int32
U32 = mybir.dt.uint32
U16 = mybir.dt.uint16
U8 = mybir.dt.uint8
FP8X4 = mybir.dt.float8_e4m3fn_x4
ACT = mybir.ActivationFunctionType
ALU = mybir.AluOpType

P = 128
S = 512
T = 2048
NT = 4
FLOPS = 3 * 2 * 512 * 512 * 512
HALF = 256


def tile_picked_twkspullbbig_none_p_kernel(tc, x_words, x_scales, d_words, d_scales, gn, w1, offs, k1, two, n1, n2, n3, out):
    nc = tc.nc
    with ExitStack() as ctx:
        keep = ctx.enter_context(tc.tile_pool(name="keep", bufs=1))
        psum4 = ctx.enter_context(tc.psum_pool(name="psum4", bufs=4))

        def load_list(src, name):
            t = keep.tile([P, S // 16], U16, name=name)
            nc.sync.dma_start(t[:], src)
            return t

        dsc = keep.tile([P, T], U8, name="dsc", align_bytes=64)
        xsc = keep.tile([P, T], U8, name="xsc", align_bytes=64)
        dw = keep.tile([P, T], U32, name="dw", align_bytes=64)
        xw = keep.tile([P, T], U32, name="xw", align_bytes=64)
        key_sc = keep.tile([P, S], U8, name="key_sc", align_bytes=64)
        nc.gpsimd.memset(dsc[:].bitcast(I32), 0)
        nc.vector.memset(xsc[:].bitcast(I32), 0)

        k1_t = load_list(k1, "k1_t")
        two_t = load_list(two, "two_t")
        nc.sync.dma_start(dsc[0:P:8, :].bitcast(I32), d_scales[0].bitcast(I32))
        for q in range(4):
            nc.scalar.dma_start(xsc[32 * q : 32 * q + 4, :].bitcast(I32), x_scales[0, 4 * q : 4 * q + 4, :].bitcast(I32))
        nc.sync.dma_start(dw[:].bitcast(I32), d_words[0].rearrange("p n t -> p (n t)").bitcast(I32))
        nc.sync.dma_start(xw[:].bitcast(I32), x_words[0].rearrange("p n t -> p (n t)").bitcast(I32))
        offs_t = load_list(offs, "offs_t")
        n2_t = load_list(n2, "n2_t")
        gain = keep.tile([P, NT], F32, name="gain")
        nc.sync.dma_start(gain[:], gn.rearrange("(p t) o -> p (t o)", t=NT))
        n1_t = load_list(n1, "n1_t")
        n3_t = load_list(n3, "n3_t")


        ksc_g = keep.tile([P, S], U8, name="ksc_g", align_bytes=64)
        nc.vector.tensor_copy(ksc_g[:], dsc[:].indirect(k1_t[:]))
        nc.vector.tensor_copy(key_sc[:].rearrange("p (t a b) -> p a t b", t=NT, b=16), ksc_g[:].rearrange("p (a b t) -> p a t b", t=NT, b=16))
        for j in range(1, 4):
            nc.scalar.dma_start(key_sc[j:P:32, :].bitcast(I32), key_sc[8 * j : P : 32, :].bitcast(I32))

        w_raw = keep.tile([P, 4, S], F32, name="ksc_g", align_bytes=64)
        nc.scalar.dma_start(w_raw[:], w1.rearrange("(p j) c -> p j c", j=4))
        kw_g = keep.tile([P, S], U32, name="kw_g", align_bytes=64)
        nc.vector.tensor_copy(kw_g[:], dw[:].indirect(k1_t[:]))
        bsc = keep.tile([P, S], U8, name="dw", align_bytes=64)
        nc.vector.tensor_copy(bsc[:], xsc[:].indirect(two_t[:]))
        key_w = keep.tile([P, S], U32, name="key_w", align_bytes=64)
        nc.vector.tensor_copy(key_w[:].rearrange("p (t a b) -> p a t b", t=NT, b=4), kw_g[:].rearrange("p (a b t) -> p a t b", t=NT, b=4))
        bw = keep.tile([P, S], U32, name="bw", align_bytes=64)
        nc.vector.tensor_copy(bw[:], xw[:].indirect(two_t[:]))

        def blk(i):
            return slice(i * P, (i + 1) * P)

        def mm(dst, lw, ls, rw, rs):
            nc.tensor.matmul_mx(out=dst, lhsT=lw.bitcast(FP8X4), lhsT_scale=ls, rhs=rw.bitcast(FP8X4), rhs_scale=rs, start=True, stop=True)

        w_q = keep.tile([P, S], U32, name="w_q", align_bytes=64)
        w_s = keep.tile([P, S], U8, name="w_s", align_bytes=64)

        b_sb = [keep.tile([P, S], F32, name="b_sb%d" % t) for t in range(NT)]
        a_sb = [keep.tile([P, S], F32, name="a_sb%d" % t) for t in range(NT)]
        stay = keep.tile([P, NT, S], F32, name="stay")
        move = keep.tile([P, NT, S], F32, name="move")
        z_bf = keep.tile([P, S, NT], BF16, name="z_bf", align_bytes=64)
        z_q = keep.tile([P, S], U32, name="z_q", align_bytes=64)
        z_s = keep.tile([P, S], U8, name="z_s", align_bytes=64)
        h_sb = [keep.tile([P, S], F32, name="h_sb%d" % t) for t in range(NT)]
        g32 = keep.tile([P, NT], F32, name="g32")
        nc.gpsimd.tensor_scalar(g32[:], gain[:], 0.03125, 0.0, ALU.mult, ALU.add)

        def gather(dst, window, lst, lo, hi, scale=1.0):
            nc.scalar.activation(out=dst, in_=window[:].indirect(lst[:, lo // 16 : hi // 16]), func=ACT.Copy, scale=scale)

        b_ps = [psum4.tile([P, S], F32, name="bh") for t in range(NT)]
        a_ps = [psum4.tile([P, S], F32, name="aa") for t in range(NT)]
        for t in range(NT):
            mm(b_ps[t][:], key_w[:, blk(t)], key_sc[:, blk(t)], bw[:], bsc[:])
        asc = keep.tile([P, S], U8, name="kw_g", align_bytes=64)
        nc.vector.tensor_copy(asc[:], xsc[:].indirect(offs_t[:]))
        aw = keep.tile([P, S], U32, name="aw", align_bytes=64)
        nc.vector.tensor_copy(aw[:], xw[:].indirect(offs_t[:]))
        for t in range(NT):
            mm(a_ps[t][:], key_w[:, blk(t)], key_sc[:, blk(t)], aw[:], asc[:])
        ident_t = keep.tile([P, P], F32, name="xw", align_bytes=64)
        ident = ident_t[:]
        make_identity(nc, ident)
        w_bf_t = keep.tile([P, NT * S], BF16, name="dw", align_bytes=64)
        w_bf = w_bf_t[:]
        for t in range(NT):
            nc.gpsimd.tensor_copy(
                w_bf[:, t * S : (t + 1) * S].rearrange("p (g e j) -> p g e j", e=16, j=4),
                w_raw[:].rearrange("p j (g t e) -> p t g e j", t=NT, e=16)[:, t],
            )
        nc.scalar.copy(b_sb[0][:], b_ps[0][:])
        for t in range(1, NT):
            nc.vector.tensor_copy(b_sb[t][:], b_ps[t][:])
        for t in range(NT):
            nc.vector.tensor_scalar(a_sb[t][:], a_ps[t][:], g32[:, t : t + 1], None, ALU.mult)

        bg = [keep.tile([P, S], F32, name="bg%d" % t) for t in range(NT)]
        dif = [psum4.tile([P, NT, P], F32, name="bh") for t in range(NT)]
        for t in range(NT):
            for lo in (0, HALF):
                gather(bg[t][:, lo : lo + HALF], b_sb[t], n2_t, lo, lo + HALF, -1.0)
            for c in range(NT):
                nc.tensor.matmul(dif[t][:, c, :], b_sb[t][:, blk(c)], ident, start=True, stop=False, is_transpose=True)
                nc.tensor.matmul(dif[t][:, c, :], bg[t][:, blk(c)], ident, start=False, stop=True, is_transpose=True)

        ag3 = keep.tile([P, S], F32, name="ag3")
        for lo in (0, HALF):
            nc.vector.tensor_copy(ag3[:, lo : lo + HALF], a_sb[3][:].indirect(n1_t[:, lo // 16 : (lo + HALF) // 16]))
        nc.vector.quantize_mx(out=w_q[:].bitcast(FP8X4), scales=w_s[:], in_=w_bf)

        th = [psum4.tile([P, S], F32, name="aa") for t in range(NT)]

        def squash(t):
            turned = keep.tile([P, NT, P], F32, name="turned%d" % t)
            nc.scalar.activation(out=turned[:], in_=dif[t][:], func=ACT.Tanh, scale=-0.03125)
            for c in range(NT):
                nc.tensor.transpose(th[t][:, blk(c)], turned[:, c, :], ident)

        def own_share(t):
            nc.vector.scalar_tensor_tensor(stay[:, t, :], th[t][:], 1.0, a_sb[t][:], ALU.subtract, ALU.mult)

        def other_share(t, cols, src):
            nc.vector.scalar_tensor_tensor(move[:, t, cols], th[t][:, cols], 1.0, src, ALU.add, ALU.mult)

        def blend(cols):
            nc.vector.tensor_tensor(
                z_bf[:, cols, :].rearrange("p (c i) t -> p c t i", i=4),
                move[:, :, cols].rearrange("p t (c i) -> p c t i", i=4),
                stay[:, :, cols].rearrange("p t (c i) -> p c t i", i=4),
                ALU.subtract,
            )

        def close(cols):
            nc.vector.quantize_mx(out=z_q[:, cols].bitcast(FP8X4), scales=z_s[:, cols], in_=z_bf[:, cols, :].rearrange("p j t -> p (j t)"))
            for t in range(NT):
                dst = hlast if (t == 0 and cols.stop == S) else hbank[t]
                mm(dst[:, cols], w_q[:, blk(t)], w_s[:, blk(t)], z_q[:, cols], z_s[:, cols])

        head, body, tail = slice(0, 128), slice(128, 384), slice(384, 512)
        for t in range(3):
            squash(t)
        ag_first = keep.tile([P, 2, P], F32, name="bg2")
        for t in range(2):
            gather(ag_first[:, t, :], a_sb[t], n1_t, 0, P)
        squash(3)
        ag = keep.tile([P, 3, S], F32, name="bg3")

        def fetch_a(t, cols):
            gather(ag[:, t, cols], a_sb[t], n1_t, cols.start, cols.stop)

        hbank = [psum4.tile([P, S], F32, name="bh") for t in range(NT)]
        hlast = psum4.tile([P, S], F32, name="aa")
        fetch_a(2, head)
        for cols in (body, tail):
            for t in range(3):
                fetch_a(t, cols)
        own_share(0)
        own_share(1)
        other_share(0, head, ag_first[:, 0, :])
        other_share(1, head, ag_first[:, 1, :])
        own_share(2)
        other_share(2, head, ag[:, 2, head])
        own_share(3)
        other_share(3, slice(0, S), ag3[:])
        blend(head)
        other_share(0, body, ag[:, 0, body])
        close(head)
        other_share(1, body, ag[:, 1, body])
        other_share(2, body, ag[:, 2, body])
        blend(body)
        other_share(0, tail, ag[:, 0, tail])
        other_share(1, tail, ag[:, 1, tail])
        close(body)
        other_share(2, tail, ag[:, 2, tail])
        blend(tail)
        close(tail)
        nc.scalar.copy(h_sb[0][:, 0:384], hbank[0][:, 0:384])
        nc.scalar.copy(h_sb[0][:, 384:S], hlast[:, 384:S])

        rows = out.rearrange("(g t e) j -> t g e j", t=NT, e=16)
        for t in range(NT):
            if t + 1 < NT:
                nc.vector.tensor_copy(h_sb[t + 1][:], hbank[t + 1][:])
            hg = keep.tile([P, S], F32, name="hg%d" % t)
            res = keep.tile([P, S], F32, name="res%d" % t)
            for lo, hi in ((0, 256), (256, 512)) if t + 1 < NT else ((0, 256), (256, 384), (384, 512)):
                nc.scalar.activation(out=hg[:, lo:hi], in_=h_sb[t][:].indirect(n3_t[:, lo // 16 : hi // 16]), func=ACT.Copy)
                nc.vector.tensor_tensor(res[:, lo:hi], hg[:, lo:hi], h_sb[t][:, lo:hi], ALU.max)
                nc.sync.dma_start(rows[t][:, :, lo:hi], res[:, lo:hi])
